import numpy as np
import ml_dtypes


def mxq(x, axis, fmt="e4m3"):
    dtype, down = {"e4m3": (ml_dtypes.float8_e4m3fn, 7), "e5m2": (ml_dtypes.float8_e5m2, 14)}[fmt]
    v = np.moveaxis(np.asarray(x, np.float32).astype(ml_dtypes.bfloat16).astype(np.float64), axis, -1)
    blocks = v.reshape(v.shape[:-1] + (-1, 32))
    amax = np.abs(blocks).max(-1, keepdims=True)
    byte = np.maximum(np.where(amax > 0, np.frexp(amax)[1] - 1 + 127, 0) - down, 1)
    scale = np.exp2(byte - 127.0)
    codes = (blocks / scale).astype(np.float32).astype(dtype).astype(np.float64)
    return np.moveaxis((codes * scale).reshape(v.shape), -1, axis)


WIDE = False


def mx_kscale(k):
    if not WIDE:
        return np.ones(k)
    levels = np.array([10, -10, 5, -5, 0])
    if k % 512:
        return np.exp2(np.random.permutation(np.resize(levels, k // 32))).repeat(32)
    a = np.empty((k // 512, 16))
    for p in range(k // 512):
        a[p, :8] = np.random.permutation(np.resize(levels, 8))
        for g in range(8):
            far = levels[np.abs(levels - a[p, g]) >= 10]
            a[p, g + 8] = far[np.random.randint(len(far))]
    return np.exp2(a.ravel()).repeat(32)


def f64(x):
    return np.asarray(x).astype(np.float64)


def striped(idx):
    return np.tile(idx.reshape(-1, 16).T, (8, 1)).astype(np.uint16)


def unstriped(offs):
    return offs[:16].T.reshape(-1).astype(np.int64)


def striped8(idx):
    return np.concatenate([x.reshape(-1, 16).T for x in idx]).astype(np.uint16)


def runs(offs, k):
    lists = np.stack([offs[16 * r : 16 * r + 16].T.reshape(-1) for r in range(8)]).astype(np.int64)
    return lists[np.arange(k) % 512 // 64]


def pack_weight(w):
    k, n = w.shape
    w = f64(np.asarray(w, np.float32).astype(ml_dtypes.bfloat16)).reshape(k // 32, 32, n)
    amax = np.abs(w).max(1)
    byte = np.clip(np.where(amax > 0, np.frexp(amax)[1] - 1 + 127 - 7, 1), 1, 254)
    scaled = (w * np.exp2(127.0 - byte)[:, None, :]).reshape(k, n).astype(np.float32)
    words = np.ascontiguousarray(scaled.reshape(k // 512, 128, 4, n).transpose(0, 1, 3, 2)).astype(ml_dtypes.float8_e4m3fn).view(np.uint8)
    return words, np.ascontiguousarray(byte.astype(np.uint8).reshape(k // 512, 16, n))


def unpack_weight(words, scales):
    g, p, n, _ = words.shape
    vals = np.ascontiguousarray(words).view(ml_dtypes.float8_e4m3fn).astype(np.float64) * np.repeat(np.exp2(scales.astype(np.float64) - 127.0), 8, axis=1)[..., None]
    return vals.transpose(0, 1, 3, 2).reshape(g * 512, n)


K, T, S, H, C = 512, 2048, 512, 512, 512


def setup_inputs():
    n = np.random.standard_normal
    s = mx_kscale(K)[:, None]
    packed_xT = pack_weight(n((K, T)) * s)
    return {
        "x_words": packed_xT[0],
        "x_scales": packed_xT[1],
        "w1": (n((K, H)) / np.sqrt(K) / s).astype(np.float32),
        "w2": (n((K, H)) / np.sqrt(K) / s).astype(np.float32),
        "gs": (np.random.uniform(0.5, 1.5, (K, 1)) / s).astype(np.float32),
        "offs": striped(np.random.permutation(T)[:S]),
        "two": striped(np.random.permutation(T)[:S]),
        "la": striped8(np.stack([np.random.permutation(S) for _ in range(8)])),
        "lb": striped8(np.stack([np.random.permutation(S) for _ in range(8)])),
        "cand": striped(np.random.permutation(T)[:C]),
    }


def reference(x_words, x_scales, w1, w2, gs, offs, two, la, lb, cand):
    x_cand = unpack_weight(x_words, x_scales)[:, unstriped(cand)]
    x_two = unpack_weight(x_words, x_scales)[:, unstriped(two)]
    c = mxq(f64(w2), 0, "e4m3").T @ x_two
    pr = np.exp(0.5 * c)
    pa = pr[np.arange(H)[:, None], runs(la, H)]
    xq = unpack_weight(x_words, x_scales)[:, unstriped(offs)]
    y = mxq(f64(w1), 0, "e4m3").T @ xq
    pb = pr[np.arange(H)[:, None], runs(lb, H)]
    z = f64(gs) * ((pa * (y[np.arange(H)[:, None], runs(la, H)]) + pb * (y[np.arange(H)[:, None], runs(lb, H)])) / (pa + pb + 1))
    return 0.0625 * ((x_cand.T @ mxq(z, 0, "e4m3")))

@@ -1,0 +1,220 @@
+from contextlib import ExitStack
+
+import concourse.mybir as mybir
+from concourse.masks import make_identity
+
+F32 = mybir.dt.float32
+BF16 = mybir.dt.bfloat16
+I32 = mybir.dt.int32
+U32 = mybir.dt.uint32
+U16 = mybir.dt.uint16
+U8 = mybir.dt.uint8
+FP8X4 = mybir.dt.float8_e4m3fn_x4
+ACT = mybir.ActivationFunctionType
+ALU = mybir.AluOpType
+
+P = 128
+PACK = 4
+K, T, S, H, C = 512, 2048, 512, 512, 512
+HALF = S // 2
+BLOCKS = S // P
+VECTOR_DEN = {(0, n, f) for n in ("la", "lb") for f in range(2)}
+FLOPS = 2 * K * H * S * 2 + 2 * K * C * S
+
+
+def tile_picked_gaussprod_none_p_kernel(
+    tc, x_words, x_scales, w1, w2, gs, offs, two, la, lb, cand, out
+):
+    nc = tc.nc
+    with ExitStack() as ctx:
+        sb = ctx.enter_context(tc.tile_pool(name="sb", bufs=1))
+        ps = ctx.enter_context(tc.psum_pool(name="ps", bufs=1))
+
+        def sbuf(name, shape, dtype):
+            return sb.tile(shape, dtype, name=name, align_bytes=64)
+
+        lists = {}
+        for name in ("two", "offs", "cand", "la", "lb"):
+            lists[name] = sbuf("list_" + name, [P, S // 16], U16)
+        xw = sbuf("xw", [P, T], U32)
+        xs = sbuf("xs", [P, T], U8)
+        gain = sbuf("gain", [P, PACK], F32)
+        raw2 = [sbuf("raw2_%d" % i, [P, PACK, H // 2], F32) for i in range(2)]
+        raw1 = [sbuf("raw1_%d" % i, [P, PACK, H // 2], F32) for i in range(2)]
+        ident = sbuf("ident", [P, P], F32)
+        one = sbuf("one", [P, 1], F32)
+        bank_a = [ps.tile([P, 512], F32, name="bank_a%d" % i) for i in range(4)]
+        bank_b = [ps.tile([P, 512], F32, name="bank_b%d" % i) for i in range(4)]
+
+        nc.vector.memset(xs[:].bitcast(I32), 0)
+        nc.vector.memset(one[:], 1.0)
+        make_identity(nc, ident[:])
+
+        w2v = w2.rearrange("(p j) c -> p j c", j=PACK)
+        w1v = w1.rearrange("(p j) c -> p j c", j=PACK)
+        nc.sync.dma_start(lists["two"][:], two)
+        for q in range(4):
+            nc.sync.dma_start(xs[32 * q : 32 * q + 4, :].bitcast(I32), x_scales[0, 4 * q : 4 * q + 4, :].bitcast(I32))
+        for half in range(2):
+            nc.sync.dma_start(raw2[half][:], w2v[:, :, 256 * half : 256 * (half + 1)])
+        nc.sync.dma_start(lists["offs"][:], offs)
+        nc.sync.dma_start(xw[:].bitcast(I32), x_words[0].rearrange("p n t -> p (n t)").bitcast(I32))
+        nc.sync.dma_start(lists["cand"][:], cand)
+        for half in range(2):
+            nc.sync.dma_start(raw1[half][:], w1v[:, :, 256 * half : 256 * (half + 1)])
+        nc.sync.dma_start(lists["la"][:], la)
+        nc.sync.dma_start(lists["lb"][:], lb)
+        nc.sync.dma_start(gain[:], gs.rearrange("(p t) o -> p (t o)", t=PACK))
+
+        def pick(name):
+            scales = sbuf("xs_" + name, [P, S], U8)
+            words = sbuf("xw_" + name, [P, S], U32)
+            return words, scales
+
+        def pick_scales(name, dst):
+            nc.vector.tensor_copy(dst[1][:], xs[:].indirect(lists[name][:]))
+
+        def pick_words(name, dst):
+            nc.vector.tensor_copy(dst[0][:], xw[:].indirect(lists[name][:]))
+
+        def deal_views(grouped, raw, half):
+            dst = grouped[:].rearrange("p (t m j) -> p m t j", t=PACK, j=PACK)[:, 64 * half : 64 * (half + 1)]
+            src = raw[half][:].rearrange("p j (m t) -> p m t j", t=PACK)
+            return dst, src
+
+        def quantise(grouped, name):
+            codes = sbuf("codes_" + name, [P, H], U32)
+            scales = sbuf("scales_" + name, [P, H], U8)
+            for t in range(PACK):
+                cols = slice(P * t, P * (t + 1))
+                nc.vector.quantize_mx(
+                    out=codes[:, cols].bitcast(FP8X4), scales=scales[:, cols], in_=grouped[:, 512 * t : 512 * (t + 1)]
+                )
+            return codes, scales
+
+        def project(banks, weights, picked):
+            for t in range(PACK):
+                cols = slice(P * t, P * (t + 1))
+                nc.tensor.matmul_mx(
+                    out=banks[t][:],
+                    lhsT=weights[0][:, cols].bitcast(FP8X4),
+                    lhsT_scale=weights[1][:, cols],
+                    rhs=picked[0][:].bitcast(FP8X4),
+                    rhs_scale=picked[1][:],
+                    start=True,
+                    stop=True,
+                )
+
+        x_two, x_idx, x_cand = pick("two"), pick("offs"), pick("cand")
+        grouped2 = sbuf("grouped2", [P, PACK * H], BF16)
+        grouped1 = sbuf("grouped1", [P, PACK * H], BF16)
+
+        pick_scales("two", x_two)
+        for half in range(2):
+            dst, src = deal_views(grouped2, raw2, half)
+            nc.scalar.copy(dst, src)
+        q2 = quantise(grouped2, "w2")
+        pick_words("two", x_two)
+        project(bank_a, q2, x_two)
+        pick_scales("offs", x_idx)
+        pick_words("offs", x_idx)
+        for half in range(2):
+            dst, src = deal_views(grouped1, raw1, half)
+            nc.vector.tensor_copy(dst, src)
+        q1 = quantise(grouped1, "w1")
+        project(bank_b, q1, x_idx)
+
+        pr = [sbuf("pr%d" % t, [P, S], F32) for t in range(PACK)]
+        hc = {}
+        for t in range(PACK):
+            if any((t, n, f) not in VECTOR_DEN for n in ("la", "lb") for f in range(2)):
+                hc[t] = sbuf("hc%d" % t, [P, S], F32)
+                nc.scalar.activation(hc[t][:], bank_a[t][:], ACT.Copy, scale=0.5)
+            nc.scalar.activation(pr[t][:], bank_a[t][:], ACT.Exp, scale=0.5)
+
+        def piece(name, half):
+            return lists[name][:, 16 * half : 16 * (half + 1)]
+
+        def add_turned(bank, t, first, second, block):
+            cols = slice(P * (block % 2), P * (block % 2 + 1))
+            dst = bank[:, P * t : P * (t + 1)]
+            nc.tensor.matmul(dst, first[:, cols], ident[:], start=True, stop=False, is_transpose=True)
+            nc.tensor.matmul(dst, second[:, cols], ident[:], start=False, stop=True, is_transpose=True)
+
+        for t in range(PACK):
+            for half in range(2):
+                got = []
+                for name in ("la", "lb"):
+                    g = sbuf("p_%s%d_%d" % (name, t, half), [P, HALF], F32)
+                    if (t, name, half) in VECTOR_DEN:
+                        nc.vector.tensor_copy(g[:], pr[t][:].indirect(piece(name, half)))
+                    else:
+                        nc.scalar.activation(g[:], hc[t][:].indirect(piece(name, half)), ACT.Exp)
+                    got.append(g)
+                for block in (2 * half, 2 * half + 1):
+                    add_turned(bank_a[block], t, got[0], got[1], block)
+
+        u = [sbuf("u%d" % t, [P, S], F32) for t in range(PACK)]
+        for t in range(PACK):
+            nc.vector.scalar_tensor_tensor(u[t][:], bank_b[t][:], gain[:, t : t + 1], pr[t][:], ALU.mult, ALU.mult)
+
+        pick_scales("cand", x_cand)
+        pick_words("cand", x_cand)
+
+        def paired(bank):
+            return bank[:].rearrange("j (u e p) -> j u p e", u=2, e=2)
+
+        def as_pairs(tile):
+            return tile[:].rearrange("j (u p e) -> j u p e", u=2, e=2)
+
+        num_bank = [bank_b[0], bank_b[1], bank_a[0], bank_a[1]]
+        word_bank = [bank_b[2], bank_b[3], bank_a[2], bank_a[3]]
+
+        def numerators(half):
+            for t in range(PACK):
+                got = []
+                for name in ("la", "lb"):
+                    g = sbuf("u_%s%d_%d" % (name, t, half), [P, HALF], F32)
+                    nc.vector.tensor_copy(g[:], u[t][:].indirect(piece(name, half)))
+                    got.append(g)
+                for block in (2 * half, 2 * half + 1):
+                    add_turned(num_bank[block], t, got[0], got[1], block)
+
+        numerators(0)
+        first = [sbuf("first%d" % b, [P, H], F32) for b in range(BLOCKS)]
+        for b in range(BLOCKS):
+            nc.scalar.activation(as_pairs(first[b]), paired(bank_a[b]), ACT.Abs_reciprocal_sqrt, bias=one[:])
+        numerators(1)
+        recip = [sbuf("recip%d" % b, [P, H], F32) for b in range(BLOCKS)]
+        for b in range(BLOCKS):
+            nc.scalar.activation(recip[b][:], first[b][:], ACT.Square)
+
+        out_v = out.rearrange("(cb p) j -> p cb j", p=P)
+        for b in range(BLOCKS):
+            zt = sbuf("zt%d" % b, [P, H], BF16)
+            nc.vector.tensor_tensor(as_pairs(zt), paired(num_bank[b]), as_pairs(recip[b]), ALU.mult)
+            words = zt[:].bitcast(F32)
+            for w in range(2):
+                nc.tensor.transpose(word_bank[b][:, P * w : P * (w + 1)], words[:, P * w : P * (w + 1)], ident[:])
+            zg = sbuf("zg%d" % b, [P, PACK * P], BF16)
+            nc.scalar.copy(
+                zg[:].bitcast(F32).rearrange("p (j w) -> p j w", w=2),
+                word_bank[b][:, 0 : 2 * P].rearrange("p (w j) -> p j w", w=2),
+            )
+            zc = sbuf("zc%d" % b, [P, P], U32)
+            zs = sbuf("zs%d" % b, [P, P], U8)
+            nc.vector.quantize_mx(out=zc[:].bitcast(FP8X4), scales=zs[:], in_=zg[:])
+            for cb in range(C // P):
+                cols = slice(P * cb, P * (cb + 1))
+                nc.tensor.matmul_mx(
+                    out=bank_b[b][:, cols],
+                    lhsT=x_cand[0][:, cols].bitcast(FP8X4),
+                    lhsT_scale=x_cand[1][:, cols],
+                    rhs=zc[:].bitcast(FP8X4),
+                    rhs_scale=zs[:],
+                    start=True,
+                    stop=True,
+                )
+            res = sbuf("res%d" % b, [P, C // P, P], F32)
+            nc.scalar.activation(res[:].rearrange("p cb j -> p (cb j)"), bank_b[b][:], ACT.Copy, scale=0.0625)
+            nc.sync.dma_start(out_v[:, :, P * b : P * (b + 1)], res[:])

@@ -18,7 +18,6 @@ PACK = 4
 K, T, S, H, C = 512, 2048, 512, 512, 512
 HALF = S // 2
 BLOCKS = S // P
-VECTOR_DEN = {(0, n, f) for n in ("la", "lb") for f in range(2)}
 FLOPS = 2 * K * H * S * 2 + 2 * K * C * S
 
 
@@ -49,6 +48,8 @@ def tile_picked_gaussprod_none_p_kernel(
         nc.vector.memset(xs[:].bitcast(I32), 0)
         nc.vector.memset(one[:], 1.0)
         make_identity(nc, ident[:])
+        warm = sbuf("warm", [P, 2], F32)
+        nc.scalar.activation(warm[:, 0:1], one[:], ACT.Exp)
 
         w2v = w2.rearrange("(p j) c -> p j c", j=PACK)
         w1v = w1.rearrange("(p j) c -> p j c", j=PACK)
@@ -57,13 +58,13 @@ def tile_picked_gaussprod_none_p_kernel(
             nc.sync.dma_start(xs[32 * q : 32 * q + 4, :].bitcast(I32), x_scales[0, 4 * q : 4 * q + 4, :].bitcast(I32))
         for half in range(2):
             nc.sync.dma_start(raw2[half][:], w2v[:, :, 256 * half : 256 * (half + 1)])
-        nc.sync.dma_start(lists["offs"][:], offs)
+        nc.sync.dma_start(lists["la"][:], la)
         nc.sync.dma_start(xw[:].bitcast(I32), x_words[0].rearrange("p n t -> p (n t)").bitcast(I32))
-        nc.sync.dma_start(lists["cand"][:], cand)
+        nc.sync.dma_start(lists["offs"][:], offs)
         for half in range(2):
             nc.sync.dma_start(raw1[half][:], w1v[:, :, 256 * half : 256 * (half + 1)])
-        nc.sync.dma_start(lists["la"][:], la)
         nc.sync.dma_start(lists["lb"][:], lb)
+        nc.sync.dma_start(lists["cand"][:], cand)
         nc.sync.dma_start(gain[:], gs.rearrange("(p t) o -> p (t o)", t=PACK))
 
         def pick(name):
@@ -112,7 +113,10 @@ def tile_picked_gaussprod_none_p_kernel(
         pick_scales("two", x_two)
         for half in range(2):
             dst, src = deal_views(grouped2, raw2, half)
-            nc.scalar.copy(dst, src)
+            if half == 0:
+                nc.scalar.copy(dst, src)
+            else:
+                nc.vector.tensor_copy(dst, src)
         q2 = quantise(grouped2, "w2")
         pick_words("two", x_two)
         project(bank_a, q2, x_two)
@@ -120,43 +124,36 @@ def tile_picked_gaussprod_none_p_kernel(
         pick_words("offs", x_idx)
         for half in range(2):
             dst, src = deal_views(grouped1, raw1, half)
-            nc.vector.tensor_copy(dst, src)
+            nc.gpsimd.tensor_scalar(dst, src, 1.0, 0.0, ALU.mult, ALU.add)
         q1 = quantise(grouped1, "w1")
         project(bank_b, q1, x_idx)
 
-        pr = [sbuf("pr%d" % t, [P, S], F32) for t in range(PACK)]
-        hc = {}
+        hp = [sbuf("hp%d" % t, [P, 2 * S], F32) for t in range(PACK)]
+        pr = [hp[t][:, S:] for t in range(PACK)]
         for t in range(PACK):
-            if any((t, n, f) not in VECTOR_DEN for n in ("la", "lb") for f in range(2)):
-                hc[t] = sbuf("hc%d" % t, [P, S], F32)
-                nc.scalar.activation(hc[t][:], bank_a[t][:], ACT.Copy, scale=0.5)
-            nc.scalar.activation(pr[t][:], bank_a[t][:], ACT.Exp, scale=0.5)
+            nc.scalar.activation(hp[t][:, :S], bank_a[t][:], ACT.Copy, scale=0.5)
+            nc.scalar.activation(pr[t], bank_a[t][:], ACT.Exp, scale=0.5)
 
         def piece(name, half):
             return lists[name][:, 16 * half : 16 * (half + 1)]
 
-        def add_turned(bank, t, first, second, block):
-            cols = slice(P * (block % 2), P * (block % 2 + 1))
+        def add_block(bank, t, first, second):
             dst = bank[:, P * t : P * (t + 1)]
-            nc.tensor.matmul(dst, first[:, cols], ident[:], start=True, stop=False, is_transpose=True)
-            nc.tensor.matmul(dst, second[:, cols], ident[:], start=False, stop=True, is_transpose=True)
+            nc.tensor.matmul(dst, first, ident[:], start=True, stop=False, is_transpose=True)
+            nc.tensor.matmul(dst, second, ident[:], start=False, stop=True, is_transpose=True)
 
         for t in range(PACK):
-            for half in range(2):
-                got = []
-                for name in ("la", "lb"):
-                    g = sbuf("p_%s%d_%d" % (name, t, half), [P, HALF], F32)
-                    if (t, name, half) in VECTOR_DEN:
-                        nc.vector.tensor_copy(g[:], pr[t][:].indirect(piece(name, half)))
-                    else:
-                        nc.scalar.activation(g[:], hc[t][:].indirect(piece(name, half)), ACT.Exp)
-                    got.append(g)
-                for block in (2 * half, 2 * half + 1):
-                    add_turned(bank_a[block], t, got[0], got[1], block)
+            got = [sbuf("p_%s%d" % (name, t), [P, S], F32) for name in ("la", "lb")]
+            for g, name in zip(got, ("la", "lb")):
+                nc.scalar.activation(g[:], hp[t][:].indirect(lists[name][:]), ACT.Exp)
+            for b in range(BLOCKS):
+                cols = slice(P * b, P * (b + 1))
+                add_block(bank_a[b], t, got[0][:, cols], got[1][:, cols])
+        nc.scalar.activation(warm[:, 1:2], got[1][:, 0:1], ACT.Abs_reciprocal_sqrt)
 
         u = [sbuf("u%d" % t, [P, S], F32) for t in range(PACK)]
         for t in range(PACK):
-            nc.vector.scalar_tensor_tensor(u[t][:], bank_b[t][:], gain[:, t : t + 1], pr[t][:], ALU.mult, ALU.mult)
+            nc.vector.scalar_tensor_tensor(u[t][:], bank_b[t][:], gain[:, t : t + 1], pr[t], ALU.mult, ALU.mult)
 
         pick_scales("cand", x_cand)
         pick_words("cand", x_cand)
@@ -170,44 +167,58 @@ def tile_picked_gaussprod_none_p_kernel(
         num_bank = [bank_b[0], bank_b[1], bank_a[0], bank_a[1]]
         word_bank = [bank_b[2], bank_b[3], bank_a[2], bank_a[3]]
 
-        def numerators(half):
-            for t in range(PACK):
-                got = []
-                for name in ("la", "lb"):
-                    g = sbuf("u_%s%d_%d" % (name, t, half), [P, HALF], F32)
-                    nc.vector.tensor_copy(g[:], u[t][:].indirect(piece(name, half)))
-                    got.append(g)
-                for block in (2 * half, 2 * half + 1):
-                    add_turned(num_bank[block], t, got[0], got[1], block)
+        def fetch(half, t):
+            room = sbuf("u_ab%d_%d" % (t, half), [P, S], F32)
+            for i, name in enumerate(("la", "lb")):
+                nc.vector.tensor_copy(room[:, HALF * i : HALF * (i + 1)], u[t][:].indirect(piece(name, half)))
+            return room
 
-        numerators(0)
-        first = [sbuf("first%d" % b, [P, H], F32) for b in range(BLOCKS)]
-        for b in range(BLOCKS):
-            nc.scalar.activation(as_pairs(first[b]), paired(bank_a[b]), ACT.Abs_reciprocal_sqrt, bias=one[:])
-        numerators(1)
+        def add_numerator(block, t, room):
+            lo = P * (block % 2)
+            add_block(num_bank[block], t, room[:, lo : lo + P], room[:, HALF + lo : HALF + lo + P])
+
+        root = [sbuf("root%d" % b, [P, H], F32) for b in range(BLOCKS)]
         recip = [sbuf("recip%d" % b, [P, H], F32) for b in range(BLOCKS)]
-        for b in range(BLOCKS):
-            nc.scalar.activation(recip[b][:], first[b][:], ACT.Square)
-
+        zt = [sbuf("zt%d" % b, [P, H], BF16) for b in range(BLOCKS)]
+        zg = [sbuf("zg%d" % b, [P, PACK * P], BF16) for b in range(BLOCKS)]
         out_v = out.rearrange("(cb p) j -> p cb j", p=P)
-        for b in range(BLOCKS):
-            zt = sbuf("zt%d" % b, [P, H], BF16)
-            nc.vector.tensor_tensor(as_pairs(zt), paired(num_bank[b]), as_pairs(recip[b]), ALU.mult)
-            words = zt[:].bitcast(F32)
+
+        def reciprocal(b):
+            nc.scalar.activation(as_pairs(root[b]), paired(bank_a[b]), ACT.Abs_reciprocal_sqrt, bias=one[:])
+            nc.scalar.activation(recip[b][:], root[b][:], ACT.Square)
+
+        def divide(b):
+            nc.vector.tensor_tensor(as_pairs(zt[b]), paired(num_bank[b]), as_pairs(recip[b]), ALU.mult)
+            words = zt[b][:].bitcast(F32)
             for w in range(2):
                 nc.tensor.transpose(word_bank[b][:, P * w : P * (w + 1)], words[:, P * w : P * (w + 1)], ident[:])
-            zg = sbuf("zg%d" % b, [P, PACK * P], BF16)
-            nc.scalar.copy(
-                zg[:].bitcast(F32).rearrange("p (j w) -> p j w", w=2),
+
+        def weave(b):
+            nc.vector.tensor_copy(
+                zg[b][:].bitcast(F32).rearrange("p (j w) -> p j w", w=2),
                 word_bank[b][:, 0 : 2 * P].rearrange("p (w j) -> p j w", w=2),
             )
+
+        def score_bank(b, cb):
+            return bank_a[0] if b == BLOCKS - 1 and cb >= 2 else bank_b[b]
+
+        def store_last():
+            b = BLOCKS - 1
+            lo = sbuf("res_lo", [P, 2, P], F32)
+            hi = sbuf("res_hi", [P, 2, P], F32)
+            nc.scalar.activation(lo[:].rearrange("p cb j -> p (cb j)"), bank_b[b][:, : 2 * P], ACT.Copy, scale=0.0625)
+            nc.vector.tensor_scalar_mul(hi[:].rearrange("p cb j -> p (cb j)"), bank_a[0][:, 2 * P :], 0.0625)
+            nc.scalar.dma_start(out_v[:, 0:2, P * b :], lo[:])
+            nc.sync.dma_start(out_v[:, 2:4, P * b :], hi[:])
+
+        def score(b):
             zc = sbuf("zc%d" % b, [P, P], U32)
             zs = sbuf("zs%d" % b, [P, P], U8)
-            nc.vector.quantize_mx(out=zc[:].bitcast(FP8X4), scales=zs[:], in_=zg[:])
+            nc.vector.quantize_mx(out=zc[:].bitcast(FP8X4), scales=zs[:], in_=zg[b][:])
             for cb in range(C // P):
                 cols = slice(P * cb, P * (cb + 1))
                 nc.tensor.matmul_mx(
-                    out=bank_b[b][:, cols],
+                    out=score_bank(b, cb)[:, cols],
                     lhsT=x_cand[0][:, cols].bitcast(FP8X4),
                     lhsT_scale=x_cand[1][:, cols],
                     rhs=zc[:].bitcast(FP8X4),
@@ -215,6 +226,38 @@ def tile_picked_gaussprod_none_p_kernel(
                     start=True,
                     stop=True,
                 )
+
+        def store(b):
             res = sbuf("res%d" % b, [P, C // P, P], F32)
             nc.scalar.activation(res[:].rearrange("p cb j -> p (cb j)"), bank_b[b][:], ACT.Copy, scale=0.0625)
             nc.sync.dma_start(out_v[:, :, P * b : P * (b + 1)], res[:])
+
+        for t in range(PACK):
+            room = fetch(0, t)
+            add_numerator(0, t, room)
+            add_numerator(1, t, room)
+        late = [fetch(1, t) for t in range(PACK)]
+        reciprocal(0)
+        for t in range(PACK):
+            add_numerator(2, t, late[t])
+        reciprocal(1)
+        divide(0)
+        for t in range(PACK):
+            add_numerator(3, t, late[t])
+        reciprocal(2)
+        reciprocal(3)
+        weave(0)
+        divide(1)
+        score(0)
+        weave(1)
+        divide(2)
+        score(1)
+        store(0)
+        weave(2)
+        divide(3)
+        score(2)
+        store(1)
+        weave(3)
+        score(3)
+        store(2)
+        store_last()

@@ -58,13 +58,13 @@ def tile_picked_gaussprod_none_p_kernel(
             nc.sync.dma_start(xs[32 * q : 32 * q + 4, :].bitcast(I32), x_scales[0, 4 * q : 4 * q + 4, :].bitcast(I32))
         for half in range(2):
             nc.sync.dma_start(raw2[half][:], w2v[:, :, 256 * half : 256 * (half + 1)])
-        nc.sync.dma_start(lists["la"][:], la)
-        nc.sync.dma_start(xw[:].bitcast(I32), x_words[0].rearrange("p n t -> p (n t)").bitcast(I32))
         nc.sync.dma_start(lists["offs"][:], offs)
+        nc.sync.dma_start(xw[:].bitcast(I32), x_words[0].rearrange("p n t -> p (n t)").bitcast(I32))
+        nc.sync.dma_start(lists["cand"][:], cand)
         for half in range(2):
             nc.sync.dma_start(raw1[half][:], w1v[:, :, 256 * half : 256 * (half + 1)])
+        nc.sync.dma_start(lists["la"][:], la)
         nc.sync.dma_start(lists["lb"][:], lb)
-        nc.sync.dma_start(lists["cand"][:], cand)
         nc.sync.dma_start(gain[:], gs.rearrange("(p t) o -> p (t o)", t=PACK))
 
         def pick(name):
@@ -83,13 +83,16 @@ def tile_picked_gaussprod_none_p_kernel(
             src = raw[half][:].rearrange("p j (m t) -> p m t j", t=PACK)
             return dst, src
 
-        def quantise(grouped, name):
+        def quantise(grouped, name, pieces):
             codes = sbuf("codes_" + name, [P, H], U32)
             scales = sbuf("scales_" + name, [P, H], U8)
-            for t in range(PACK):
-                cols = slice(P * t, P * (t + 1))
+            width = H // pieces
+            for i in range(pieces):
+                cols = slice(width * i, width * (i + 1))
                 nc.vector.quantize_mx(
-                    out=codes[:, cols].bitcast(FP8X4), scales=scales[:, cols], in_=grouped[:, 512 * t : 512 * (t + 1)]
+                    out=codes[:, cols].bitcast(FP8X4),
+                    scales=scales[:, cols],
+                    in_=grouped[:, PACK * width * i : PACK * width * (i + 1)],
                 )
             return codes, scales
 
@@ -113,11 +116,8 @@ def tile_picked_gaussprod_none_p_kernel(
         pick_scales("two", x_two)
         for half in range(2):
             dst, src = deal_views(grouped2, raw2, half)
-            if half == 0:
-                nc.scalar.copy(dst, src)
-            else:
-                nc.vector.tensor_copy(dst, src)
-        q2 = quantise(grouped2, "w2")
+            nc.scalar.copy(dst, src)
+        q2 = quantise(grouped2, "w2", 4)
         pick_words("two", x_two)
         project(bank_a, q2, x_two)
         pick_scales("offs", x_idx)
@@ -125,14 +125,14 @@ def tile_picked_gaussprod_none_p_kernel(
         for half in range(2):
             dst, src = deal_views(grouped1, raw1, half)
             nc.gpsimd.tensor_scalar(dst, src, 1.0, 0.0, ALU.mult, ALU.add)
-        q1 = quantise(grouped1, "w1")
+        q1 = quantise(grouped1, "w1", 2)
         project(bank_b, q1, x_idx)
 
-        hp = [sbuf("hp%d" % t, [P, 2 * S], F32) for t in range(PACK)]
-        pr = [hp[t][:, S:] for t in range(PACK)]
+        hp = [sbuf("hp%d" % t, [P, 2 * S if t else S], F32) for t in range(PACK)]
+        pr = [hp[t][:, S:] if t else sbuf("pr0", [P, S], F32)[:] for t in range(PACK)]
         for t in range(PACK):
-            nc.scalar.activation(hp[t][:, :S], bank_a[t][:], ACT.Copy, scale=0.5)
             nc.scalar.activation(pr[t], bank_a[t][:], ACT.Exp, scale=0.5)
+            nc.scalar.activation(hp[t][:, :S], bank_a[t][:], ACT.Copy, scale=0.5)
 
         def piece(name, half):
             return lists[name][:, 16 * half : 16 * (half + 1)]
@@ -144,8 +144,14 @@ def tile_picked_gaussprod_none_p_kernel(
 
         for t in range(PACK):
             got = [sbuf("p_%s%d" % (name, t), [P, S], F32) for name in ("la", "lb")]
-            for g, name in zip(got, ("la", "lb")):
-                nc.scalar.activation(g[:], hp[t][:].indirect(lists[name][:]), ACT.Exp)
+            if t == 0:
+                for half in range(2):
+                    cols = slice(HALF * half, HALF * (half + 1))
+                    nc.vector.tensor_copy(got[0][:, cols], pr[0].indirect(piece("la", half)))
+                    nc.scalar.activation(got[1][:, cols], hp[0][:].indirect(piece("lb", half)), ACT.Exp)
+            else:
+                for g, name in zip(got, ("la", "lb")):
+                    nc.scalar.activation(g[:], hp[t][:].indirect(lists[name][:]), ACT.Exp)
             for b in range(BLOCKS):
                 cols = slice(P * b, P * (b + 1))
                 add_block(bank_a[b], t, got[0][:, cols], got[1][:, cols])
@@ -164,11 +170,10 @@ def tile_picked_gaussprod_none_p_kernel(
         def as_pairs(tile):
             return tile[:].rearrange("j (u p e) -> j u p e", u=2, e=2)
 
-        num_bank = [bank_b[0], bank_b[1], bank_a[0], bank_a[1]]
-        word_bank = [bank_b[2], bank_b[3], bank_a[2], bank_a[3]]
+        num_bank = bank_b
+        word_bank = bank_a
 
-        def fetch(half, t):
-            room = sbuf("u_ab%d_%d" % (t, half), [P, S], F32)
+        def fetch(half, t, room):
             for i, name in enumerate(("la", "lb")):
                 nc.vector.tensor_copy(room[:, HALF * i : HALF * (i + 1)], u[t][:].indirect(piece(name, half)))
             return room
@@ -179,22 +184,38 @@ def tile_picked_gaussprod_none_p_kernel(
 
         root = [sbuf("root%d" % b, [P, H], F32) for b in range(BLOCKS)]
         recip = [sbuf("recip%d" % b, [P, H], F32) for b in range(BLOCKS)]
-        zt = [sbuf("zt%d" % b, [P, H], BF16) for b in range(BLOCKS)]
         zg = [sbuf("zg%d" % b, [P, PACK * P], BF16) for b in range(BLOCKS)]
         out_v = out.rearrange("(cb p) j -> p cb j", p=P)
 
+        def parts(b):
+            return [slice(0, 1), slice(1, 2)] if b == BLOCKS - 1 else [slice(0, 2)]
+
         def reciprocal(b):
-            nc.scalar.activation(as_pairs(root[b]), paired(bank_a[b]), ACT.Abs_reciprocal_sqrt, bias=one[:])
-            nc.scalar.activation(recip[b][:], root[b][:], ACT.Square)
+            for w in parts(b):
+                cols = slice(HALF * w.start, HALF * w.stop)
+                nc.scalar.activation(as_pairs(root[b])[:, w], paired(bank_a[b])[:, w], ACT.Abs_reciprocal_sqrt, bias=one[:])
+                if b == 0:
+                    nc.gpsimd.tensor_tensor(recip[b][:], root[b][:], root[b][:], ALU.mult)
+                else:
+                    nc.scalar.activation(recip[b][:, cols], root[b][:, cols], ACT.Square)
 
         def divide(b):
-            nc.vector.tensor_tensor(as_pairs(zt[b]), paired(num_bank[b]), as_pairs(recip[b]), ALU.mult)
-            words = zt[b][:].bitcast(F32)
-            for w in range(2):
-                nc.tensor.transpose(word_bank[b][:, P * w : P * (w + 1)], words[:, P * w : P * (w + 1)], ident[:])
+            for w in parts(b):
+                half_z = sbuf("zt%d_%d" % (b, w.start), [P, HALF * (w.stop - w.start)], BF16)
+                nc.vector.tensor_tensor(
+                    half_z[:].rearrange("j (u p e) -> j u p e", p=P, e=2),
+                    paired(num_bank[b])[:, w],
+                    as_pairs(recip[b])[:, w],
+                    ALU.mult,
+                )
+                words = half_z[:].bitcast(F32)
+                for i in range(w.start, w.stop):
+                    lo = P * (i - w.start)
+                    nc.tensor.transpose(word_bank[b][:, P * i : P * (i + 1)], words[:, lo : lo + P], ident[:])
 
         def weave(b):
-            nc.vector.tensor_copy(
+            copy = nc.vector.tensor_copy if b == 0 else nc.scalar.copy
+            copy(
                 zg[b][:].bitcast(F32).rearrange("p (j w) -> p j w", w=2),
                 word_bank[b][:, 0 : 2 * P].rearrange("p (w j) -> p j w", w=2),
             )
@@ -229,35 +250,36 @@ def tile_picked_gaussprod_none_p_kernel(
 
         def store(b):
             res = sbuf("res%d" % b, [P, C // P, P], F32)
-            nc.scalar.activation(res[:].rearrange("p cb j -> p (cb j)"), bank_b[b][:], ACT.Copy, scale=0.0625)
+            flat = res[:].rearrange("p cb j -> p (cb j)")
+            if b % 2 == 0:
+                nc.vector.tensor_scalar_mul(flat, bank_b[b][:], 0.0625)
+            else:
+                nc.scalar.activation(flat, bank_b[b][:], ACT.Copy, scale=0.0625)
             nc.sync.dma_start(out_v[:, :, P * b : P * (b + 1)], res[:])
 
         for t in range(PACK):
-            room = fetch(0, t)
+            room = fetch(0, t, sbuf("u_ab%d_0" % t, [P, S], F32))
             add_numerator(0, t, room)
             add_numerator(1, t, room)
-        late = [fetch(1, t) for t in range(PACK)]
-        reciprocal(0)
         for t in range(PACK):
-            add_numerator(2, t, late[t])
-        reciprocal(1)
+            room = fetch(1, t, got[1] if t == 2 else sbuf("u_ab%d_1" % t, [P, S], F32))
+            add_numerator(2, t, room)
+            add_numerator(3, t, room)
+        for b in range(BLOCKS):
+            reciprocal(b)
         divide(0)
-        for t in range(PACK):
-            add_numerator(3, t, late[t])
-        reciprocal(2)
-        reciprocal(3)
-        weave(0)
         divide(1)
+        weave(0)
+        divide(2)
         score(0)
         weave(1)
-        divide(2)
-        score(1)
-        store(0)
-        weave(2)
         divide(3)
+        score(1)
+        weave(2)
+        store(0)
         score(2)
-        store(1)
         weave(3)
         score(3)
+        store(1)
         store(2)
         store_last()

@@ -15,9 +15,13 @@ ALU = mybir.AluOpType
 
 P = 128
 PACK = 4
+GROUP = 16
 K, T, S, H, C = 512, 2048, 512, 512, 512
 HALF = S // 2
 BLOCKS = S // P
+LAST = BLOCKS - 1
+PAIRS = PACK // 2
+OUT_SCALE = 0.0625
 FLOPS = 2 * K * H * S * 2 + 2 * K * C * S
 
 
@@ -34,56 +38,57 @@ def tile_picked_gaussprod_none_p_kernel(
 
         lists = {}
         for name in ("two", "offs", "cand", "la", "lb"):
-            lists[name] = sbuf("list_" + name, [P, S // 16], U16)
-        xw = sbuf("xw", [P, T], U32)
-        xs = sbuf("xs", [P, T], U8)
+            lists[name] = sbuf("list_" + name, [P, S // GROUP], U16)
+        table_words = sbuf("table_words", [P, T], U32)
+        table_scales = sbuf("table_scales", [P, T], U8)
         gain = sbuf("gain", [P, PACK], F32)
-        raw2 = [sbuf("raw2_%d" % i, [P, PACK, H // 2], F32) for i in range(2)]
-        raw1 = [sbuf("raw1_%d" % i, [P, PACK, H // 2], F32) for i in range(2)]
+        raw2 = [sbuf("raw2_%d" % half, [P, PACK, H // 2], F32) for half in range(2)]
+        raw1 = [sbuf("raw1_%d" % half, [P, PACK, H // 2], F32) for half in range(2)]
         ident = sbuf("ident", [P, P], F32)
         one = sbuf("one", [P, 1], F32)
-        bank_a = [ps.tile([P, 512], F32, name="bank_a%d" % i) for i in range(4)]
-        bank_b = [ps.tile([P, 512], F32, name="bank_b%d" % i) for i in range(4)]
+        bank_a = [ps.tile([P, S], F32, name="bank_a%d" % i) for i in range(PACK)]
+        bank_b = [ps.tile([P, S], F32, name="bank_b%d" % i) for i in range(PACK)]
 
-        nc.vector.memset(xs[:].bitcast(I32), 0)
+        nc.vector.memset(table_scales[:].bitcast(I32), 0)
         nc.vector.memset(one[:], 1.0)
         make_identity(nc, ident[:])
-        warm = sbuf("warm", [P, 2], F32)
-        nc.scalar.activation(warm[:, 0:1], one[:], ACT.Exp)
 
-        w2v = w2.rearrange("(p j) c -> p j c", j=PACK)
-        w1v = w1.rearrange("(p j) c -> p j c", j=PACK)
+        w2_rows = w2.rearrange("(p j) c -> p j c", j=PACK)
+        w1_rows = w1.rearrange("(p j) c -> p j c", j=PACK)
         nc.sync.dma_start(lists["two"][:], two)
         for q in range(4):
-            nc.sync.dma_start(xs[32 * q : 32 * q + 4, :].bitcast(I32), x_scales[0, 4 * q : 4 * q + 4, :].bitcast(I32))
+            nc.sync.dma_start(
+                table_scales[32 * q : 32 * q + 4, :].bitcast(I32), x_scales[0, 4 * q : 4 * q + 4, :].bitcast(I32)
+            )
         for half in range(2):
-            nc.sync.dma_start(raw2[half][:], w2v[:, :, 256 * half : 256 * (half + 1)])
+            nc.sync.dma_start(raw2[half][:], w2_rows[:, :, H // 2 * half : H // 2 * (half + 1)])
         nc.sync.dma_start(lists["offs"][:], offs)
-        nc.sync.dma_start(xw[:].bitcast(I32), x_words[0].rearrange("p n t -> p (n t)").bitcast(I32))
+        nc.sync.dma_start(table_words[:].bitcast(I32), x_words[0].rearrange("p n j -> p (n j)").bitcast(I32))
         nc.sync.dma_start(lists["cand"][:], cand)
         for half in range(2):
-            nc.sync.dma_start(raw1[half][:], w1v[:, :, 256 * half : 256 * (half + 1)])
+            nc.sync.dma_start(raw1[half][:], w1_rows[:, :, H // 2 * half : H // 2 * (half + 1)])
         nc.sync.dma_start(lists["la"][:], la)
         nc.sync.dma_start(lists["lb"][:], lb)
         nc.sync.dma_start(gain[:], gs.rearrange("(p t) o -> p (t o)", t=PACK))
 
-        def pick(name):
-            scales = sbuf("xs_" + name, [P, S], U8)
-            words = sbuf("xw_" + name, [P, S], U32)
-            return words, scales
+        picked_scales = {}
+        picked_words = {}
+        for name in ("two", "offs", "cand"):
+            picked_scales[name] = sbuf("scales_" + name, [P, S], U8)
+            picked_words[name] = sbuf("words_" + name, [P, S], U32)
 
-        def pick_scales(name, dst):
-            nc.vector.tensor_copy(dst[1][:], xs[:].indirect(lists[name][:]))
+        def pick_scales(name):
+            nc.vector.tensor_copy(picked_scales[name][:], table_scales[:].indirect(lists[name][:]))
 
-        def pick_words(name, dst):
-            nc.vector.tensor_copy(dst[0][:], xw[:].indirect(lists[name][:]))
+        def pick_words(name):
+            nc.vector.tensor_copy(picked_words[name][:], table_words[:].indirect(lists[name][:]))
 
         def deal_views(grouped, raw, half):
-            dst = grouped[:].rearrange("p (t m j) -> p m t j", t=PACK, j=PACK)[:, 64 * half : 64 * (half + 1)]
+            dst = grouped[:].rearrange("p (t m j) -> p m t j", t=PACK, j=PACK)
             src = raw[half][:].rearrange("p j (m t) -> p m t j", t=PACK)
-            return dst, src
+            return dst[:, P // 2 * half : P // 2 * (half + 1)], src
 
-        def quantise(grouped, name, pieces):
+        def quantise_weight(grouped, name, pieces):
             codes = sbuf("codes_" + name, [P, H], U32)
             scales = sbuf("scales_" + name, [P, H], U8)
             width = H // pieces
@@ -96,189 +101,189 @@ def tile_picked_gaussprod_none_p_kernel(
                 )
             return codes, scales
 
-        def project(banks, weights, picked):
+        def project(banks, codes, scales, name):
             for t in range(PACK):
                 cols = slice(P * t, P * (t + 1))
                 nc.tensor.matmul_mx(
                     out=banks[t][:],
-                    lhsT=weights[0][:, cols].bitcast(FP8X4),
-                    lhsT_scale=weights[1][:, cols],
-                    rhs=picked[0][:].bitcast(FP8X4),
-                    rhs_scale=picked[1][:],
+                    lhsT=codes[:, cols].bitcast(FP8X4),
+                    lhsT_scale=scales[:, cols],
+                    rhs=picked_words[name][:].bitcast(FP8X4),
+                    rhs_scale=picked_scales[name][:],
                     start=True,
                     stop=True,
                 )
 
-        x_two, x_idx, x_cand = pick("two"), pick("offs"), pick("cand")
         grouped2 = sbuf("grouped2", [P, PACK * H], BF16)
         grouped1 = sbuf("grouped1", [P, PACK * H], BF16)
 
-        pick_scales("two", x_two)
+        pick_scales("two")
         for half in range(2):
             dst, src = deal_views(grouped2, raw2, half)
             nc.scalar.copy(dst, src)
-        q2 = quantise(grouped2, "w2", 4)
-        pick_words("two", x_two)
-        project(bank_a, q2, x_two)
-        pick_scales("offs", x_idx)
-        pick_words("offs", x_idx)
+        codes2, scales2 = quantise_weight(grouped2, "w2", PACK)
+        pick_words("two")
+        project(bank_a, codes2, scales2, "two")
+
+        pick_scales("offs")
+        pick_words("offs")
         for half in range(2):
             dst, src = deal_views(grouped1, raw1, half)
             nc.gpsimd.tensor_scalar(dst, src, 1.0, 0.0, ALU.mult, ALU.add)
-        q1 = quantise(grouped1, "w1", 2)
-        project(bank_b, q1, x_idx)
+        codes1, scales1 = quantise_weight(grouped1, "w1", 2)
+        project(bank_b, codes1, scales1, "offs")
 
-        hp = [sbuf("hp%d" % t, [P, 2 * S if t else S], F32) for t in range(PACK)]
-        pr = [hp[t][:, S:] if t else sbuf("pr0", [P, S], F32)[:] for t in range(PACK)]
+        half_c = [sbuf("half_c%d" % t, [P, 2 * S if t else S], F32) for t in range(PACK)]
+        pr = [half_c[t][:, S:] if t else sbuf("pr0", [P, S], F32)[:] for t in range(PACK)]
         for t in range(PACK):
             nc.scalar.activation(pr[t], bank_a[t][:], ACT.Exp, scale=0.5)
-            nc.scalar.activation(hp[t][:, :S], bank_a[t][:], ACT.Copy, scale=0.5)
+            nc.scalar.activation(half_c[t][:, :S], bank_a[t][:], ACT.Copy, scale=0.5)
 
-        def piece(name, half):
-            return lists[name][:, 16 * half : 16 * (half + 1)]
+        def half_list(name, half):
+            return lists[name][:, HALF // GROUP * half : HALF // GROUP * (half + 1)]
 
-        def add_block(bank, t, first, second):
+        def add_turned(bank, t, first, second):
             dst = bank[:, P * t : P * (t + 1)]
             nc.tensor.matmul(dst, first, ident[:], start=True, stop=False, is_transpose=True)
             nc.tensor.matmul(dst, second, ident[:], start=False, stop=True, is_transpose=True)
 
+        pa, pb = [], []
         for t in range(PACK):
-            got = [sbuf("p_%s%d" % (name, t), [P, S], F32) for name in ("la", "lb")]
+            pa.append(sbuf("pa%d" % t, [P, S], F32))
+            pb.append(sbuf("pb%d" % t, [P, S], F32))
             if t == 0:
                 for half in range(2):
                     cols = slice(HALF * half, HALF * (half + 1))
-                    nc.vector.tensor_copy(got[0][:, cols], pr[0].indirect(piece("la", half)))
-                    nc.scalar.activation(got[1][:, cols], hp[0][:].indirect(piece("lb", half)), ACT.Exp)
+                    nc.vector.tensor_copy(pa[t][:, cols], pr[t].indirect(half_list("la", half)))
+                    nc.scalar.activation(pb[t][:, cols], half_c[t][:].indirect(half_list("lb", half)), ACT.Exp)
             else:
-                for g, name in zip(got, ("la", "lb")):
-                    nc.scalar.activation(g[:], hp[t][:].indirect(lists[name][:]), ACT.Exp)
+                nc.scalar.activation(pa[t][:], half_c[t][:].indirect(lists["la"][:]), ACT.Exp)
+                nc.scalar.activation(pb[t][:], half_c[t][:].indirect(lists["lb"][:]), ACT.Exp)
             for b in range(BLOCKS):
                 cols = slice(P * b, P * (b + 1))
-                add_block(bank_a[b], t, got[0][:, cols], got[1][:, cols])
-        nc.scalar.activation(warm[:, 1:2], got[1][:, 0:1], ACT.Abs_reciprocal_sqrt)
+                add_turned(bank_a[b], t, pa[t][:, cols], pb[t][:, cols])
 
-        u = [sbuf("u%d" % t, [P, S], F32) for t in range(PACK)]
+        weighted = [sbuf("weighted%d" % t, [P, S], F32) for t in range(PACK)]
         for t in range(PACK):
-            nc.vector.scalar_tensor_tensor(u[t][:], bank_b[t][:], gain[:, t : t + 1], pr[t], ALU.mult, ALU.mult)
+            nc.vector.scalar_tensor_tensor(weighted[t][:], bank_b[t][:], gain[:, t : t + 1], pr[t], ALU.mult, ALU.mult)
 
-        pick_scales("cand", x_cand)
-        pick_words("cand", x_cand)
+        pick_scales("cand")
+        pick_words("cand")
 
-        def paired(bank):
-            return bank[:].rearrange("j (u e p) -> j u p e", u=2, e=2)
+        for half in range(2):
+            for t in range(PACK):
+                if half == 1 and t == PACK - 2:
+                    fetched = pb[PACK - 1]
+                else:
+                    fetched = sbuf("fetched%d_%d" % (t, half), [P, S], F32)
+                for i, name in enumerate(("la", "lb")):
+                    nc.vector.tensor_copy(
+                        fetched[:, HALF * i : HALF * (i + 1)], weighted[t][:].indirect(half_list(name, half))
+                    )
+                for i in range(HALF // P):
+                    lo = P * i
+                    add_turned(
+                        bank_b[HALF // P * half + i], t, fetched[:, lo : lo + P], fetched[:, HALF + lo : HALF + lo + P]
+                    )
 
-        def as_pairs(tile):
-            return tile[:].rearrange("j (u p e) -> j u p e", u=2, e=2)
+        def bank_by_pairs(bank):
+            return bank[:].rearrange("j (u e p) -> j u p e", u=PAIRS, e=2)
 
-        num_bank = bank_b
-        word_bank = bank_a
+        def tile_by_pairs(tile):
+            return tile[:].rearrange("j (u p e) -> j u p e", p=P, e=2)
 
-        def fetch(half, t, room):
-            for i, name in enumerate(("la", "lb")):
-                nc.vector.tensor_copy(room[:, HALF * i : HALF * (i + 1)], u[t][:].indirect(piece(name, half)))
-            return room
-
-        def add_numerator(block, t, room):
-            lo = P * (block % 2)
-            add_block(num_bank[block], t, room[:, lo : lo + P], room[:, HALF + lo : HALF + lo + P])
+        def pair_ranges(b):
+            return [slice(u, u + 1) for u in range(PAIRS)] if b == LAST else [slice(0, PAIRS)]
 
         root = [sbuf("root%d" % b, [P, H], F32) for b in range(BLOCKS)]
         recip = [sbuf("recip%d" % b, [P, H], F32) for b in range(BLOCKS)]
-        zg = [sbuf("zg%d" % b, [P, PACK * P], BF16) for b in range(BLOCKS)]
-        out_v = out.rearrange("(cb p) j -> p cb j", p=P)
-
-        def parts(b):
-            return [slice(0, 1), slice(1, 2)] if b == BLOCKS - 1 else [slice(0, 2)]
+        z_grouped = [sbuf("z_grouped%d" % b, [P, PACK * P], BF16) for b in range(BLOCKS)]
+        out_rows = out.rearrange("(cb p) j -> p cb j", p=P)
 
         def reciprocal(b):
-            for w in parts(b):
-                cols = slice(HALF * w.start, HALF * w.stop)
-                nc.scalar.activation(as_pairs(root[b])[:, w], paired(bank_a[b])[:, w], ACT.Abs_reciprocal_sqrt, bias=one[:])
-                if b == 0:
+            for us in pair_ranges(b):
+                cols = slice(2 * P * us.start, 2 * P * us.stop)
+                nc.scalar.activation(
+                    tile_by_pairs(root[b])[:, us], bank_by_pairs(bank_a[b])[:, us], ACT.Abs_reciprocal_sqrt, bias=one[:]
+                )
+                if b == 1:
                     nc.gpsimd.tensor_tensor(recip[b][:], root[b][:], root[b][:], ALU.mult)
                 else:
                     nc.scalar.activation(recip[b][:, cols], root[b][:, cols], ACT.Square)
 
         def divide(b):
-            for w in parts(b):
-                half_z = sbuf("zt%d_%d" % (b, w.start), [P, HALF * (w.stop - w.start)], BF16)
+            for us in pair_ranges(b):
+                z_turned = sbuf("z_turned%d_%d" % (b, us.start), [P, 2 * P * (us.stop - us.start)], BF16)
                 nc.vector.tensor_tensor(
-                    half_z[:].rearrange("j (u p e) -> j u p e", p=P, e=2),
-                    paired(num_bank[b])[:, w],
-                    as_pairs(recip[b])[:, w],
-                    ALU.mult,
+                    tile_by_pairs(z_turned), bank_by_pairs(bank_b[b])[:, us], tile_by_pairs(recip[b])[:, us], ALU.mult
                 )
-                words = half_z[:].bitcast(F32)
-                for i in range(w.start, w.stop):
-                    lo = P * (i - w.start)
-                    nc.tensor.transpose(word_bank[b][:, P * i : P * (i + 1)], words[:, lo : lo + P], ident[:])
+                z_words = z_turned[:].bitcast(F32)
+                for u in range(us.start, us.stop):
+                    lo = P * (u - us.start)
+                    nc.tensor.transpose(bank_a[b][:, P * u : P * (u + 1)], z_words[:, lo : lo + P], ident[:])
 
-        def weave(b):
+        def interleave(b):
             copy = nc.vector.tensor_copy if b == 0 else nc.scalar.copy
             copy(
-                zg[b][:].bitcast(F32).rearrange("p (j w) -> p j w", w=2),
-                word_bank[b][:, 0 : 2 * P].rearrange("p (w j) -> p j w", w=2),
+                z_grouped[b][:].bitcast(F32).rearrange("p (j u) -> p j u", u=PAIRS),
+                bank_a[b][:, 0 : PAIRS * P].rearrange("p (u j) -> p j u", u=PAIRS),
             )
 
         def score_bank(b, cb):
-            return bank_a[0] if b == BLOCKS - 1 and cb >= 2 else bank_b[b]
-
-        def store_last():
-            b = BLOCKS - 1
-            lo = sbuf("res_lo", [P, 2, P], F32)
-            hi = sbuf("res_hi", [P, 2, P], F32)
-            nc.scalar.activation(lo[:].rearrange("p cb j -> p (cb j)"), bank_b[b][:, : 2 * P], ACT.Copy, scale=0.0625)
-            nc.vector.tensor_scalar_mul(hi[:].rearrange("p cb j -> p (cb j)"), bank_a[0][:, 2 * P :], 0.0625)
-            nc.scalar.dma_start(out_v[:, 0:2, P * b :], lo[:])
-            nc.sync.dma_start(out_v[:, 2:4, P * b :], hi[:])
+            return bank_a[0] if b == LAST and cb >= C // P // 2 else bank_b[b]
 
         def score(b):
-            zc = sbuf("zc%d" % b, [P, P], U32)
-            zs = sbuf("zs%d" % b, [P, P], U8)
-            nc.vector.quantize_mx(out=zc[:].bitcast(FP8X4), scales=zs[:], in_=zg[b][:])
+            z_codes = sbuf("z_codes%d" % b, [P, P], U32)
+            z_scales = sbuf("z_scales%d" % b, [P, P], U8)
+            nc.vector.quantize_mx(out=z_codes[:].bitcast(FP8X4), scales=z_scales[:], in_=z_grouped[b][:])
             for cb in range(C // P):
                 cols = slice(P * cb, P * (cb + 1))
                 nc.tensor.matmul_mx(
                     out=score_bank(b, cb)[:, cols],
-                    lhsT=x_cand[0][:, cols].bitcast(FP8X4),
-                    lhsT_scale=x_cand[1][:, cols],
-                    rhs=zc[:].bitcast(FP8X4),
-                    rhs_scale=zs[:],
+                    lhsT=picked_words["cand"][:, cols].bitcast(FP8X4),
+                    lhsT_scale=picked_scales["cand"][:, cols],
+                    rhs=z_codes[:].bitcast(FP8X4),
+                    rhs_scale=z_scales[:],
                     start=True,
                     stop=True,
                 )
 
         def store(b):
-            res = sbuf("res%d" % b, [P, C // P, P], F32)
-            flat = res[:].rearrange("p cb j -> p (cb j)")
+            result = sbuf("result%d" % b, [P, C // P, P], F32)
+            flat = result[:].rearrange("p cb j -> p (cb j)")
             if b % 2 == 0:
-                nc.vector.tensor_scalar_mul(flat, bank_b[b][:], 0.0625)
+                nc.vector.tensor_scalar_mul(flat, bank_b[b][:], OUT_SCALE)
             else:
-                nc.scalar.activation(flat, bank_b[b][:], ACT.Copy, scale=0.0625)
-            nc.sync.dma_start(out_v[:, :, P * b : P * (b + 1)], res[:])
+                nc.scalar.activation(flat, bank_b[b][:], ACT.Copy, scale=OUT_SCALE)
+            nc.sync.dma_start(out_rows[:, :, P * b : P * (b + 1)], result[:])
 
-        for t in range(PACK):
-            room = fetch(0, t, sbuf("u_ab%d_0" % t, [P, S], F32))
-            add_numerator(0, t, room)
-            add_numerator(1, t, room)
-        for t in range(PACK):
-            room = fetch(1, t, got[1] if t == 2 else sbuf("u_ab%d_1" % t, [P, S], F32))
-            add_numerator(2, t, room)
-            add_numerator(3, t, room)
-        for b in range(BLOCKS):
+        def store_last():
+            mid = C // P // 2
+            low = sbuf("result_low", [P, mid, P], F32)
+            high = sbuf("result_high", [P, mid, P], F32)
+            nc.scalar.activation(
+                low[:].rearrange("p cb j -> p (cb j)"), score_bank(LAST, 0)[:, : mid * P], ACT.Copy, scale=OUT_SCALE
+            )
+            nc.vector.tensor_scalar_mul(
+                high[:].rearrange("p cb j -> p (cb j)"), score_bank(LAST, mid)[:, mid * P :], OUT_SCALE
+            )
+            nc.scalar.dma_start(out_rows[:, :mid, P * LAST :], low[:])
+            nc.sync.dma_start(out_rows[:, mid:, P * LAST :], high[:])
+
+        for b in (1, 0, 2, 3):
             reciprocal(b)
         divide(0)
         divide(1)
-        weave(0)
+        interleave(0)
         divide(2)
         score(0)
-        weave(1)
+        interleave(1)
         divide(3)
         score(1)
-        weave(2)
+        interleave(2)
         store(0)
         score(2)
-        weave(3)
+        interleave(3)
         score(3)
         store(1)
         store(2)

from contextlib import ExitStack

import concourse.mybir as mybir
from concourse.masks import make_identity

F32 = mybir.dt.float32
BF16 = mybir.dt.bfloat16
I32 = mybir.dt.int32
U32 = mybir.dt.uint32
U16 = mybir.dt.uint16
U8 = mybir.dt.uint8
FP8X4 = mybir.dt.float8_e4m3fn_x4
ACT = mybir.ActivationFunctionType
ALU = mybir.AluOpType

P = 128
PACK = 4
GROUP = 16
K, T, S, H, C = 512, 2048, 512, 512, 512
HALF = S // 2
BLOCKS = S // P
LAST = BLOCKS - 1
PAIRS = PACK // 2
OUT_SCALE = 0.0625
FLOPS = 2 * K * H * S * 2 + 2 * K * C * S


def tile_picked_gaussprod_none_p_kernel(
    tc, x_words, x_scales, w1, w2, gs, offs, two, la, lb, cand, out
):
    nc = tc.nc
    with ExitStack() as ctx:
        sb = ctx.enter_context(tc.tile_pool(name="sb", bufs=1))
        ps = ctx.enter_context(tc.psum_pool(name="ps", bufs=1))

        def sbuf(name, shape, dtype):
            return sb.tile(shape, dtype, name=name, align_bytes=64)

        lists = {}
        for name in ("two", "offs", "cand", "la", "lb"):
            lists[name] = sbuf("list_" + name, [P, S // GROUP], U16)
        table_words = sbuf("table_words", [P, T], U32)
        table_scales = sbuf("table_scales", [P, T], U8)
        gain = sbuf("gain", [P, PACK], F32)
        raw2 = [sbuf("raw2_%d" % half, [P, PACK, H // 2], F32) for half in range(2)]
        raw1 = [sbuf("raw1_%d" % half, [P, PACK, H // 2], F32) for half in range(2)]
        ident = sbuf("ident", [P, P], F32)
        one = sbuf("one", [P, 1], F32)
        bank_a = [ps.tile([P, S], F32, name="bank_a%d" % i) for i in range(PACK)]
        bank_b = [ps.tile([P, S], F32, name="bank_b%d" % i) for i in range(PACK)]

        nc.vector.memset(table_scales[:].bitcast(I32), 0)
        nc.vector.memset(one[:], 1.0)
        make_identity(nc, ident[:])

        w2_rows = w2.rearrange("(p j) c -> p j c", j=PACK)
        w1_rows = w1.rearrange("(p j) c -> p j c", j=PACK)
        nc.sync.dma_start(lists["two"][:], two)
        for q in range(4):
            nc.sync.dma_start(
                table_scales[32 * q : 32 * q + 4, :].bitcast(I32), x_scales[0, 4 * q : 4 * q + 4, :].bitcast(I32)
            )
        for half in range(2):
            nc.sync.dma_start(raw2[half][:], w2_rows[:, :, H // 2 * half : H // 2 * (half + 1)])
        nc.sync.dma_start(lists["offs"][:], offs)
        nc.sync.dma_start(table_words[:].bitcast(I32), x_words[0].rearrange("p n j -> p (n j)").bitcast(I32))
        nc.sync.dma_start(lists["cand"][:], cand)
        for half in range(2):
            nc.sync.dma_start(raw1[half][:], w1_rows[:, :, H // 2 * half : H // 2 * (half + 1)])
        nc.sync.dma_start(lists["la"][:], la)
        nc.sync.dma_start(lists["lb"][:], lb)
        nc.sync.dma_start(gain[:], gs.rearrange("(p t) o -> p (t o)", t=PACK))

        picked_scales = {}
        picked_words = {}
        for name in ("two", "offs", "cand"):
            picked_scales[name] = sbuf("scales_" + name, [P, S], U8)
            picked_words[name] = sbuf("words_" + name, [P, S], U32)

        def pick_scales(name):
            nc.vector.tensor_copy(picked_scales[name][:], table_scales[:].indirect(lists[name][:]))

        def pick_words(name):
            nc.vector.tensor_copy(picked_words[name][:], table_words[:].indirect(lists[name][:]))

        def deal_views(grouped, raw, half):
            dst = grouped[:].rearrange("p (t m j) -> p m t j", t=PACK, j=PACK)
            src = raw[half][:].rearrange("p j (m t) -> p m t j", t=PACK)
            return dst[:, P // 2 * half : P // 2 * (half + 1)], src

        def quantise_weight(grouped, name, pieces):
            codes = sbuf("codes_" + name, [P, H], U32)
            scales = sbuf("scales_" + name, [P, H], U8)
            width = H // pieces
            for i in range(pieces):
                cols = slice(width * i, width * (i + 1))
                nc.vector.quantize_mx(
                    out=codes[:, cols].bitcast(FP8X4),
                    scales=scales[:, cols],
                    in_=grouped[:, PACK * width * i : PACK * width * (i + 1)],
                )
            return codes, scales

        def project(banks, codes, scales, name):
            for t in range(PACK):
                cols = slice(P * t, P * (t + 1))
                nc.tensor.matmul_mx(
                    out=banks[t][:],
                    lhsT=codes[:, cols].bitcast(FP8X4),
                    lhsT_scale=scales[:, cols],
                    rhs=picked_words[name][:].bitcast(FP8X4),
                    rhs_scale=picked_scales[name][:],
                    start=True,
                    stop=True,
                )

        grouped2 = sbuf("grouped2", [P, PACK * H], BF16)
        grouped1 = sbuf("grouped1", [P, PACK * H], BF16)

        pick_scales("two")
        for half in range(2):
            dst, src = deal_views(grouped2, raw2, half)
            nc.scalar.copy(dst, src)
        codes2, scales2 = quantise_weight(grouped2, "w2", PACK)
        pick_words("two")
        project(bank_a, codes2, scales2, "two")

        pick_scales("offs")
        pick_words("offs")
        for half in range(2):
            dst, src = deal_views(grouped1, raw1, half)
            nc.gpsimd.tensor_scalar(dst, src, 1.0, 0.0, ALU.mult, ALU.add)
        codes1, scales1 = quantise_weight(grouped1, "w1", 2)
        project(bank_b, codes1, scales1, "offs")

        half_c = [sbuf("half_c%d" % t, [P, 2 * S if t else S], F32) for t in range(PACK)]
        pr = [half_c[t][:, S:] if t else sbuf("pr0", [P, S], F32)[:] for t in range(PACK)]
        for t in range(PACK):
            nc.scalar.activation(pr[t], bank_a[t][:], ACT.Exp, scale=0.5)
            nc.scalar.activation(half_c[t][:, :S], bank_a[t][:], ACT.Copy, scale=0.5)

        def half_list(name, half):
            return lists[name][:, HALF // GROUP * half : HALF // GROUP * (half + 1)]

        def add_turned(bank, t, first, second):
            dst = bank[:, P * t : P * (t + 1)]
            nc.tensor.matmul(dst, first, ident[:], start=True, stop=False, is_transpose=True)
            nc.tensor.matmul(dst, second, ident[:], start=False, stop=True, is_transpose=True)

        pa, pb = [], []
        for t in range(PACK):
            pa.append(sbuf("pa%d" % t, [P, S], F32))
            pb.append(sbuf("pb%d" % t, [P, S], F32))
            if t == 0:
                for half in range(2):
                    cols = slice(HALF * half, HALF * (half + 1))
                    nc.vector.tensor_copy(pa[t][:, cols], pr[t].indirect(half_list("la", half)))
                    nc.scalar.activation(pb[t][:, cols], half_c[t][:].indirect(half_list("lb", half)), ACT.Exp)
            else:
                nc.scalar.activation(pa[t][:], half_c[t][:].indirect(lists["la"][:]), ACT.Exp)
                nc.scalar.activation(pb[t][:], half_c[t][:].indirect(lists["lb"][:]), ACT.Exp)
            for b in range(BLOCKS):
                cols = slice(P * b, P * (b + 1))
                add_turned(bank_a[b], t, pa[t][:, cols], pb[t][:, cols])

        weighted = [sbuf("weighted%d" % t, [P, S], F32) for t in range(PACK)]
        for t in range(PACK):
            nc.vector.scalar_tensor_tensor(weighted[t][:], bank_b[t][:], gain[:, t : t + 1], pr[t], ALU.mult, ALU.mult)

        pick_scales("cand")
        pick_words("cand")

        for half in range(2):
            for t in range(PACK):
                if half == 1 and t == PACK - 2:
                    fetched = pb[PACK - 1]
                else:
                    fetched = sbuf("fetched%d_%d" % (t, half), [P, S], F32)
                for i, name in enumerate(("la", "lb")):
                    nc.vector.tensor_copy(
                        fetched[:, HALF * i : HALF * (i + 1)], weighted[t][:].indirect(half_list(name, half))
                    )
                for i in range(HALF // P):
                    lo = P * i
                    add_turned(
                        bank_b[HALF // P * half + i], t, fetched[:, lo : lo + P], fetched[:, HALF + lo : HALF + lo + P]
                    )

        def bank_by_pairs(bank):
            return bank[:].rearrange("j (u e p) -> j u p e", u=PAIRS, e=2)

        def tile_by_pairs(tile):
            return tile[:].rearrange("j (u p e) -> j u p e", p=P, e=2)

        def pair_ranges(b):
            return [slice(u, u + 1) for u in range(PAIRS)] if b == LAST else [slice(0, PAIRS)]

        root = [sbuf("root%d" % b, [P, H], F32) for b in range(BLOCKS)]
        recip = [sbuf("recip%d" % b, [P, H], F32) for b in range(BLOCKS)]
        z_grouped = [sbuf("z_grouped%d" % b, [P, PACK * P], BF16) for b in range(BLOCKS)]
        out_rows = out.rearrange("(cb p) j -> p cb j", p=P)

        def reciprocal(b):
            for us in pair_ranges(b):
                cols = slice(2 * P * us.start, 2 * P * us.stop)
                nc.scalar.activation(
                    tile_by_pairs(root[b])[:, us], bank_by_pairs(bank_a[b])[:, us], ACT.Abs_reciprocal_sqrt, bias=one[:]
                )
                if b == 1:
                    nc.gpsimd.tensor_tensor(recip[b][:], root[b][:], root[b][:], ALU.mult)
                else:
                    nc.scalar.activation(recip[b][:, cols], root[b][:, cols], ACT.Square)

        def divide(b):
            for us in pair_ranges(b):
                z_turned = sbuf("z_turned%d_%d" % (b, us.start), [P, 2 * P * (us.stop - us.start)], BF16)
                nc.vector.tensor_tensor(
                    tile_by_pairs(z_turned), bank_by_pairs(bank_b[b])[:, us], tile_by_pairs(recip[b])[:, us], ALU.mult
                )
                z_words = z_turned[:].bitcast(F32)
                for u in range(us.start, us.stop):
                    lo = P * (u - us.start)
                    nc.tensor.transpose(bank_a[b][:, P * u : P * (u + 1)], z_words[:, lo : lo + P], ident[:])

        def interleave(b):
            copy = nc.vector.tensor_copy if b == 0 else nc.scalar.copy
            copy(
                z_grouped[b][:].bitcast(F32).rearrange("p (j u) -> p j u", u=PAIRS),
                bank_a[b][:, 0 : PAIRS * P].rearrange("p (u j) -> p j u", u=PAIRS),
            )

        def score_bank(b, cb):
            return bank_a[0] if b == LAST and cb >= C // P // 2 else bank_b[b]

        def score(b):
            z_codes = sbuf("z_codes%d" % b, [P, P], U32)
            z_scales = sbuf("z_scales%d" % b, [P, P], U8)
            nc.vector.quantize_mx(out=z_codes[:].bitcast(FP8X4), scales=z_scales[:], in_=z_grouped[b][:])
            for cb in range(C // P):
                cols = slice(P * cb, P * (cb + 1))
                nc.tensor.matmul_mx(
                    out=score_bank(b, cb)[:, cols],
                    lhsT=picked_words["cand"][:, cols].bitcast(FP8X4),
                    lhsT_scale=picked_scales["cand"][:, cols],
                    rhs=z_codes[:].bitcast(FP8X4),
                    rhs_scale=z_scales[:],
                    start=True,
                    stop=True,
                )

        def store(b):
            result = sbuf("result%d" % b, [P, C // P, P], F32)
            flat = result[:].rearrange("p cb j -> p (cb j)")
            if b % 2 == 0:
                nc.vector.tensor_scalar_mul(flat, bank_b[b][:], OUT_SCALE)
            else:
                nc.scalar.activation(flat, bank_b[b][:], ACT.Copy, scale=OUT_SCALE)
            nc.sync.dma_start(out_rows[:, :, P * b : P * (b + 1)], result[:])

        def store_last():
            mid = C // P // 2
            low = sbuf("result_low", [P, mid, P], F32)
            high = sbuf("result_high", [P, mid, P], F32)
            nc.scalar.activation(
                low[:].rearrange("p cb j -> p (cb j)"), score_bank(LAST, 0)[:, : mid * P], ACT.Copy, scale=OUT_SCALE
            )
            nc.vector.tensor_scalar_mul(
                high[:].rearrange("p cb j -> p (cb j)"), score_bank(LAST, mid)[:, mid * P :], OUT_SCALE
            )
            nc.scalar.dma_start(out_rows[:, :mid, P * LAST :], low[:])
            nc.sync.dma_start(out_rows[:, mid:, P * LAST :], high[:])

        for b in (1, 0, 2, 3):
            reciprocal(b)
        divide(0)
        divide(1)
        interleave(0)
        divide(2)
        score(0)
        interleave(1)
        divide(3)
        score(1)
        interleave(2)
        store(0)
        score(2)
        interleave(3)
        score(3)
        store(1)
        store(2)
        store_last()
